import numpy as np
import ml_dtypes


def mxq(x, axis, fmt="e4m3"):
    dtype, down = {"e4m3": (ml_dtypes.float8_e4m3fn, 7), "e5m2": (ml_dtypes.float8_e5m2, 14)}[fmt]
    v = np.moveaxis(np.asarray(x, np.float32).astype(ml_dtypes.bfloat16).astype(np.float64), axis, -1)
    blocks = v.reshape(v.shape[:-1] + (-1, 32))
    amax = np.abs(blocks).max(-1, keepdims=True)
    byte = np.maximum(np.where(amax > 0, np.frexp(amax)[1] - 1 + 127, 0) - down, 1)
    scale = np.exp2(byte - 127.0)
    codes = (blocks / scale).astype(np.float32).astype(dtype).astype(np.float64)
    return np.moveaxis((codes * scale).reshape(v.shape), -1, axis)


WIDE = False


def mx_kscale(k):
    if not WIDE:
        return np.ones(k)
    levels = np.array([10, -10, 5, -5, 0])
    if k % 512:
        return np.exp2(np.random.permutation(np.resize(levels, k // 32))).repeat(32)
    a = np.empty((k // 512, 16))
    for p in range(k // 512):
        a[p, :8] = np.random.permutation(np.resize(levels, 8))
        for g in range(8):
            far = levels[np.abs(levels - a[p, g]) >= 10]
            a[p, g + 8] = far[np.random.randint(len(far))]
    return np.exp2(a.ravel()).repeat(32)


def f64(x):
    return np.asarray(x).astype(np.float64)


def striped8(idx):
    return np.concatenate([v.reshape(-1, 16).T for v in idx]).astype(np.uint16)


def unstriped8(offs):
    return np.stack([offs[16 * g:16 * g + 16].T.reshape(-1) for g in range(8)]).astype(np.int64)


E2M1 = np.array([0.0, 0.5, 1.0, 1.5, 2.0, 3.0, 4.0, 6.0, -0.0, -0.5, -1.0, -1.5, -2.0, -3.0, -4.0, -6.0])


def pack_weight(w, fmt):
    k, n = w.shape
    w = f64(np.asarray(w, np.float32).astype(ml_dtypes.bfloat16)).reshape(k // 32, 32, n)
    amax = np.abs(w).max(1)
    if fmt == "e4m3":
        byte = np.frexp(amax)[1] - 1 + 127 - 7
    else:
        mant, ex = np.frexp(amax / 6.0)
        byte = np.where(mant > 0.5, ex, ex - 1) + 127
    byte = np.clip(np.where(amax > 0, byte, 1), 1, 254)
    scaled = (w * np.exp2(127.0 - byte)[:, None, :]).reshape(k, n).astype(np.float32)
    by_word = np.ascontiguousarray(scaled.reshape(k // 512, 128, 4, n).transpose(0, 1, 3, 2))
    if fmt == "e4m3":
        words = by_word.astype(ml_dtypes.float8_e4m3fn).view(np.uint8)
    else:
        c = by_word.astype(ml_dtypes.float4_e2m1fn).view(np.uint8) & 0xF
        words = (c[..., 0::2] | (c[..., 1::2] << 4)).reshape(k // 512, 128, 2 * n)
    return np.ascontiguousarray(words), np.ascontiguousarray(byte.astype(np.uint8).reshape(k // 512, 16, n))


def unpack_weight(words, scales, fmt):
    g, _, n = scales.shape
    words = np.ascontiguousarray(words).reshape(g, 128, n, -1)
    if fmt == "e4m3":
        vals = words.view(ml_dtypes.float8_e4m3fn).astype(np.float64)
    else:
        nib = np.empty((g, 128, n, 4), np.uint8)
        nib[..., 0::2] = words & 0xF
        nib[..., 1::2] = words >> 4
        vals = E2M1[nib]
    vals = vals * np.repeat(np.exp2(scales.astype(np.float64) - 127.0), 8, axis=1)[..., None]
    return vals.transpose(0, 1, 3, 2).reshape(g * 512, n)


def silu(v):
    return v / (1.0 + np.exp(-np.maximum(v, -700.0)))


K, M, T, S = 512, 512, 1024, 512


def setup_inputs():
    n = np.random.standard_normal
    s = mx_kscale(K)[:, None]
    p_w = pack_weight(n((K, M)) / np.sqrt(K) / s, "e2m1")
    return {
        "xT": (n((K, T)) * s).astype(np.float32),
        "w_words": p_w[0],
        "w_scales": p_w[1],
        "wgt": np.repeat(np.random.uniform(0.5, 2.0, (8, S)), 16, axis=0).astype(np.float32),
        "b": (0.3 * n(512)).astype(np.float32),
        "wgo": np.repeat(np.random.uniform(0.5, 2.0, (8, S)), 16, axis=0).astype(np.float32),
        "offs": striped8(np.stack([np.random.permutation(T)[:S] for _ in range(8)])),
        "offs2": striped8(np.stack([np.random.permutation(T)[:S] for _ in range(8)])),
    }


def reference(xT, w_words, w_scales, wgt, b, wgo, offs, offs2):
    idx = unstriped8(offs)
    group = np.arange(K) % 512 // 64
    xg = f64(wgt)[np.arange(K) // 4 % 128] * f64(xT)[np.arange(K)[:, None], idx[group]]
    xT_ = mxq(xg, 0, "e4m3")
    w_ = unpack_weight(w_words, w_scales, "e2m1")
    y = w_.T @ xT_
    place = unstriped8(offs2)[np.arange(M) % 128 // 16]
    out = np.zeros((M, T))
    out[np.arange(M)[:, None], place] = f64(wgo)[np.arange(M) % 128] * (silu(y + f64(b)[:, None]))
    return out

@@ -1,0 +1,120 @@
+from contextlib import ExitStack
+
+import concourse.mybir as mybir
+
+K, M, T, S = 512, 512, 1024, 512
+FLOPS = 2 * K * M * S
+
+F32 = mybir.dt.float32
+BF16 = mybir.dt.bfloat16
+I32 = mybir.dt.int32
+U32 = mybir.dt.uint32
+U16 = mybir.dt.uint16
+U8 = mybir.dt.uint8
+E4M3X4 = mybir.dt.float8_e4m3fn_x4
+E2M1X4 = mybir.dt.float4_e2m1fn_x4
+MULT = mybir.AluOpType.mult
+SILU = mybir.ActivationFunctionType.Silu
+
+P = 128
+H = S // 2
+A_SCALAR = 128
+
+
+def tile_list_hboth_silu_kernel(tc, xT, w_words, w_scales, wgt, b, wgo, offs, offs2, out):
+    nc = tc.nc
+    with ExitStack() as ctx:
+        lists = ctx.enter_context(tc.tile_pool(name="lists", bufs=1))
+        keep = ctx.enter_context(tc.tile_pool(name="keep", bufs=1))
+        psum = ctx.enter_context(tc.psum_pool(name="psum", bufs=1))
+
+        offs_t = lists.tile([P, S // 16], U16, name="offs_t")
+        offs2_t = lists.tile([P, S // 16], U16, name="offs2_t")
+        planes = [keep.tile([P, T], F32, name=f"plane{i}") for i in range(4)]
+        wgt_t = [keep.tile([P, H], F32, name=f"wgt{h}") for h in range(2)]
+        wgo_t = [keep.tile([P, H], F32, name=f"wgo{h}") for h in range(2)]
+        picked = [keep.tile([P, 4, H], F32, name=f"picked{h}") for h in range(2)]
+        grouped = [keep.tile([P, H, 4], BF16, name=f"grouped{h}", align_bytes=64) for h in range(2)]
+        codes = [keep.tile([P, H], U32, name=f"codes{h}", align_bytes=64) for h in range(2)]
+        scales = [keep.tile([P, H], U8, name=f"scales{h}", align_bytes=64) for h in range(2)]
+        w_t = keep.tile([P, 2 * M], U8, name="w_t", align_bytes=64)
+        ws_t = keep.tile([P, M], U8, name="ws_t", align_bytes=64)
+        b_t = keep.tile([P, 4], F32, name="b_t")
+        dummy = keep.tile([P, 1], F32, name="dummy")
+        wins = [keep.tile([P, T], F32, name=f"win{n}") for n in range(4)]
+        acts = [[keep.tile([P, H], F32, name=f"act{h}_{n}") for n in range(4)] for h in range(2)]
+        accs = [[psum.tile([P, H], F32, name=f"acc{h}_{n}") for n in range(4)] for h in range(2)]
+
+        x_rows = xT.rearrange("(p i) t -> p i t", i=4)
+        nc.sync.dma_start(out=offs_t[:], in_=offs)
+        nc.sync.dma_start(out=wgt_t[0][:], in_=wgt[:, 0:H])
+        nc.sync.dma_start(out=planes[0][:], in_=x_rows[:, 0, :])
+        nc.sync.dma_start(out=wgt_t[1][:], in_=wgt[:, H:S])
+        nc.sync.dma_start(out=planes[1][:], in_=x_rows[:, 1, :])
+        nc.sync.dma_start(out=planes[2][:], in_=x_rows[:, 2, :])
+        nc.sync.dma_start(out=planes[3][:], in_=x_rows[:, 3, :])
+
+        nc.vector.memset(dummy[:], 0.0)
+        nc.vector.memset(ws_t[:].bitcast(I32), 0)
+        nc.scalar.activation(dummy[:], dummy[:], SILU)
+        nc.sync.dma_start(out=w_t[:].bitcast(I32), in_=w_words[0].bitcast(I32))
+        for q in range(4):
+            nc.sync.dma_start(
+                out=ws_t[32 * q : 32 * q + 4, :].bitcast(I32),
+                in_=w_scales[0][4 * q : 4 * q + 4, :].bitcast(I32),
+            )
+        with nc.allow_non_contiguous_dma(reason="bias, one element a partition"):
+            nc.sync.dma_start(out=b_t[:], in_=b.rearrange("(c p) -> p c", p=P))
+        nc.sync.dma_start(out=offs2_t[:], in_=offs2)
+        nc.sync.dma_start(out=wgo_t[0][:], in_=wgo[:, 0:H])
+        nc.sync.dma_start(out=wgo_t[1][:], in_=wgo[:, H:S])
+        for n in range(4):
+            (nc.vector if n < 2 else nc.gpsimd).memset(wins[n][:], 0.0)
+
+        def gather(h, i):
+            cols = slice(h * H // 16, (h + 1) * H // 16)
+            nc.vector.tensor_tensor(picked[h][:, i, :], planes[i][:].indirect(offs_t[:, cols]), wgt_t[h][:], MULT)
+
+        def interleave(engine_copy, h, c0, c1):
+            engine_copy(grouped[h][:, c0:c1, :], picked[h][:, :, c0:c1].rearrange("p i c -> p c i"))
+
+        def quantize(h):
+            nc.vector.quantize_mx(
+                out=codes[h][:].bitcast(E4M3X4), scales=scales[h][:], in_=grouped[h][:].rearrange("p c i -> p (c i)")
+            )
+
+        def multiply(h):
+            for n in range(4):
+                nc.tensor.matmul_mx(
+                    out=accs[h][n][:],
+                    lhsT=w_t[:, 2 * P * n : 2 * P * (n + 1)].bitcast(E2M1X4),
+                    lhsT_scale=ws_t[:, P * n : P * (n + 1)],
+                    rhs=codes[h][:].bitcast(E4M3X4),
+                    rhs_scale=scales[h][:],
+                    start=True,
+                    stop=True,
+                )
+                nc.scalar.activation(acts[h][n][:], accs[h][n][:], SILU, bias=b_t[:, n : n + 1])
+
+        def scatter(h, n):
+            cols = slice(h * H // 16, (h + 1) * H // 16)
+            nc.vector.tensor_tensor(wins[n][:].indirect(offs2_t[:, cols]), acts[h][n][:], wgo_t[h][:], MULT)
+
+        for h, i in ((0, 0), (1, 0), (0, 1), (1, 1), (0, 2), (0, 3)):
+            gather(h, i)
+        interleave(nc.scalar.copy, 0, 0, A_SCALAR)
+        interleave(nc.vector.tensor_copy, 0, A_SCALAR, H)
+        gather(1, 2)
+        quantize(0)
+        multiply(0)
+        gather(1, 3)
+        interleave(nc.scalar.copy, 1, 0, H)
+        scatter(0, 0)
+        scatter(0, 1)
+        quantize(1)
+        multiply(1)
+        scatter(0, 2)
+        scatter(0, 3)
+        for n in range(4):
+            scatter(1, n)
+            nc.sync.dma_start(out=out[P * n : P * (n + 1), :], in_=wins[n][:])

@@ -18,7 +18,6 @@ SILU = mybir.ActivationFunctionType.Silu
 
 P = 128
 H = S // 2
-A_SCALAR = 128
 
 
 def tile_list_hboth_silu_kernel(tc, xT, w_words, w_scales, wgt, b, wgo, offs, offs2, out):
@@ -71,12 +70,14 @@ def tile_list_hboth_silu_kernel(tc, xT, w_words, w_scales, wgt, b, wgo, offs, of
         for n in range(4):
             (nc.vector if n < 2 else nc.gpsimd).memset(wins[n][:], 0.0)
 
-        def gather(h, i):
-            cols = slice(h * H // 16, (h + 1) * H // 16)
-            nc.vector.tensor_tensor(picked[h][:, i, :], planes[i][:].indirect(offs_t[:, cols]), wgt_t[h][:], MULT)
+        def gather(h, i, j0=0, j1=H):
+            cols = slice((h * H + j0) // 16, (h * H + j1) // 16)
+            nc.vector.tensor_tensor(
+                picked[h][:, i, j0:j1], planes[i][:].indirect(offs_t[:, cols]), wgt_t[h][:, j0:j1], MULT
+            )
 
-        def interleave(engine_copy, h, c0, c1):
-            engine_copy(grouped[h][:, c0:c1, :], picked[h][:, :, c0:c1].rearrange("p i c -> p c i"))
+        def interleave(h, i0, i1, j0=0, j1=H):
+            nc.scalar.copy(grouped[h][:, j0:j1, i0:i1], picked[h][:, i0:i1, j0:j1].rearrange("p i c -> p c i"))
 
         def quantize(h):
             nc.vector.quantize_mx(
@@ -100,15 +101,21 @@ def tile_list_hboth_silu_kernel(tc, xT, w_words, w_scales, wgt, b, wgo, offs, of
             cols = slice(h * H // 16, (h + 1) * H // 16)
             nc.vector.tensor_tensor(wins[n][:].indirect(offs2_t[:, cols]), acts[h][n][:], wgo_t[h][:], MULT)
 
-        for h, i in ((0, 0), (1, 0), (0, 1), (1, 1), (0, 2), (0, 3)):
-            gather(h, i)
-        interleave(nc.scalar.copy, 0, 0, A_SCALAR)
-        interleave(nc.vector.tensor_copy, 0, A_SCALAR, H)
-        gather(1, 2)
+        gather(0, 0)
+        gather(1, 0)
+        gather(0, 1)
+        interleave(0, 0, 2)
+        gather(0, 2)
+        gather(0, 3, 0, H // 2)
+        interleave(0, 2, 4, 0, H // 2)
+        gather(0, 3, H // 2, H)
+        interleave(0, 2, 4, H // 2, H)
+        gather(1, 1)
         quantize(0)
         multiply(0)
+        gather(1, 2)
         gather(1, 3)
-        interleave(nc.scalar.copy, 1, 0, H)
+        interleave(1, 0, 4)
         scatter(0, 0)
         scatter(0, 1)
         quantize(1)

@@ -79,9 +79,11 @@ def tile_list_hboth_silu_kernel(tc, xT, w_words, w_scales, wgt, b, wgo, offs, of
         def interleave(h, i0, i1, j0=0, j1=H):
             nc.scalar.copy(grouped[h][:, j0:j1, i0:i1], picked[h][:, i0:i1, j0:j1].rearrange("p i c -> p c i"))
 
-        def quantize(h):
+        def quantize(h, j0=0, j1=H):
             nc.vector.quantize_mx(
-                out=codes[h][:].bitcast(E4M3X4), scales=scales[h][:], in_=grouped[h][:].rearrange("p c i -> p (c i)")
+                out=codes[h][:, j0:j1].bitcast(E4M3X4),
+                scales=scales[h][:, j0:j1],
+                in_=grouped[h][:, j0:j1, :].rearrange("p c i -> p (c i)"),
             )
 
         def multiply(h):
@@ -105,13 +107,14 @@ def tile_list_hboth_silu_kernel(tc, xT, w_words, w_scales, wgt, b, wgo, offs, of
         gather(1, 0)
         gather(0, 1)
         interleave(0, 0, 2)
+        gather(1, 1)
         gather(0, 2)
         gather(0, 3, 0, H // 2)
         interleave(0, 2, 4, 0, H // 2)
         gather(0, 3, H // 2, H)
         interleave(0, 2, 4, H // 2, H)
-        gather(1, 1)
-        quantize(0)
+        quantize(0, 0, H // 2)
+        quantize(0, H // 2, H)
         multiply(0)
         gather(1, 2)
         gather(1, 3)

from contextlib import ExitStack

import concourse.mybir as mybir

K, M, T, S = 512, 512, 1024, 512
FLOPS = 2 * K * M * S

F32 = mybir.dt.float32
BF16 = mybir.dt.bfloat16
I32 = mybir.dt.int32
U32 = mybir.dt.uint32
U16 = mybir.dt.uint16
U8 = mybir.dt.uint8
E4M3X4 = mybir.dt.float8_e4m3fn_x4
E2M1X4 = mybir.dt.float4_e2m1fn_x4
MULT = mybir.AluOpType.mult
SILU = mybir.ActivationFunctionType.Silu

P = 128
H = S // 2


def tile_list_hboth_silu_kernel(tc, xT, w_words, w_scales, wgt, b, wgo, offs, offs2, out):
    nc = tc.nc
    with ExitStack() as ctx:
        lists = ctx.enter_context(tc.tile_pool(name="lists", bufs=1))
        keep = ctx.enter_context(tc.tile_pool(name="keep", bufs=1))
        psum = ctx.enter_context(tc.psum_pool(name="psum", bufs=1))

        offs_t = lists.tile([P, S // 16], U16, name="offs_t")
        offs2_t = lists.tile([P, S // 16], U16, name="offs2_t")
        planes = [keep.tile([P, T], F32, name=f"plane{i}") for i in range(4)]
        wgt_t = [keep.tile([P, H], F32, name=f"wgt{h}") for h in range(2)]
        wgo_t = [keep.tile([P, H], F32, name=f"wgo{h}") for h in range(2)]
        picked = [keep.tile([P, 4, H], F32, name=f"picked{h}") for h in range(2)]
        grouped = [keep.tile([P, H, 4], BF16, name=f"grouped{h}", align_bytes=64) for h in range(2)]
        codes = [keep.tile([P, H], U32, name=f"codes{h}", align_bytes=64) for h in range(2)]
        scales = [keep.tile([P, H], U8, name=f"scales{h}", align_bytes=64) for h in range(2)]
        w_t = keep.tile([P, 2 * M], U8, name="w_t", align_bytes=64)
        ws_t = keep.tile([P, M], U8, name="ws_t", align_bytes=64)
        b_t = keep.tile([P, 4], F32, name="b_t")
        dummy = keep.tile([P, 1], F32, name="dummy")
        wins = [keep.tile([P, T], F32, name=f"win{n}") for n in range(4)]
        acts = [[keep.tile([P, H], F32, name=f"act{h}_{n}") for n in range(4)] for h in range(2)]
        accs = [[psum.tile([P, H], F32, name=f"acc{h}_{n}") for n in range(4)] for h in range(2)]

        x_rows = xT.rearrange("(p i) t -> p i t", i=4)
        nc.sync.dma_start(out=offs_t[:], in_=offs)
        nc.sync.dma_start(out=wgt_t[0][:], in_=wgt[:, 0:H])
        nc.sync.dma_start(out=planes[0][:], in_=x_rows[:, 0, :])
        nc.sync.dma_start(out=wgt_t[1][:], in_=wgt[:, H:S])
        nc.sync.dma_start(out=planes[1][:], in_=x_rows[:, 1, :])
        nc.sync.dma_start(out=planes[2][:], in_=x_rows[:, 2, :])
        nc.sync.dma_start(out=planes[3][:], in_=x_rows[:, 3, :])

        nc.vector.memset(dummy[:], 0.0)
        nc.vector.memset(ws_t[:].bitcast(I32), 0)
        nc.scalar.activation(dummy[:], dummy[:], SILU)
        nc.sync.dma_start(out=w_t[:].bitcast(I32), in_=w_words[0].bitcast(I32))
        for q in range(4):
            nc.sync.dma_start(
                out=ws_t[32 * q : 32 * q + 4, :].bitcast(I32),
                in_=w_scales[0][4 * q : 4 * q + 4, :].bitcast(I32),
            )
        with nc.allow_non_contiguous_dma(reason="bias, one element a partition"):
            nc.sync.dma_start(out=b_t[:], in_=b.rearrange("(c p) -> p c", p=P))
        nc.sync.dma_start(out=offs2_t[:], in_=offs2)
        nc.sync.dma_start(out=wgo_t[0][:], in_=wgo[:, 0:H])
        nc.sync.dma_start(out=wgo_t[1][:], in_=wgo[:, H:S])
        for n in range(4):
            (nc.vector if n < 2 else nc.gpsimd).memset(wins[n][:], 0.0)

        def gather(h, i, j0=0, j1=H):
            cols = slice((h * H + j0) // 16, (h * H + j1) // 16)
            nc.vector.tensor_tensor(
                picked[h][:, i, j0:j1], planes[i][:].indirect(offs_t[:, cols]), wgt_t[h][:, j0:j1], MULT
            )

        def interleave(h, i0, i1, j0=0, j1=H):
            nc.scalar.copy(grouped[h][:, j0:j1, i0:i1], picked[h][:, i0:i1, j0:j1].rearrange("p i c -> p c i"))

        def quantize(h, j0=0, j1=H):
            nc.vector.quantize_mx(
                out=codes[h][:, j0:j1].bitcast(E4M3X4),
                scales=scales[h][:, j0:j1],
                in_=grouped[h][:, j0:j1, :].rearrange("p c i -> p (c i)"),
            )

        def multiply(h):
            for n in range(4):
                nc.tensor.matmul_mx(
                    out=accs[h][n][:],
                    lhsT=w_t[:, 2 * P * n : 2 * P * (n + 1)].bitcast(E2M1X4),
                    lhsT_scale=ws_t[:, P * n : P * (n + 1)],
                    rhs=codes[h][:].bitcast(E4M3X4),
                    rhs_scale=scales[h][:],
                    start=True,
                    stop=True,
                )
                nc.scalar.activation(acts[h][n][:], accs[h][n][:], SILU, bias=b_t[:, n : n + 1])

        def scatter(h, n):
            cols = slice(h * H // 16, (h + 1) * H // 16)
            nc.vector.tensor_tensor(wins[n][:].indirect(offs2_t[:, cols]), acts[h][n][:], wgo_t[h][:], MULT)

        gather(0, 0)
        gather(1, 0)
        gather(0, 1)
        interleave(0, 0, 2)
        gather(1, 1)
        gather(0, 2)
        gather(0, 3, 0, H // 2)
        interleave(0, 2, 4, 0, H // 2)
        gather(0, 3, H // 2, H)
        interleave(0, 2, 4, H // 2, H)
        quantize(0, 0, H // 2)
        quantize(0, H // 2, H)
        multiply(0)
        gather(1, 2)
        gather(1, 3)
        interleave(1, 0, 4)
        scatter(0, 0)
        scatter(0, 1)
        quantize(1)
        multiply(1)
        scatter(0, 2)
        scatter(0, 3)
        for n in range(4):
            scatter(1, n)
            nc.sync.dma_start(out=out[P * n : P * (n + 1), :], in_=wins[n][:])
